import numpy as np
CORES = [24,25,26,27,28,29,30,31,0,8,16]
N = 11
ROOT = 10
def setup_inputs(rng):
    return {"x": rng.standard_normal((N, 128, 1024), dtype=np.float32)}
def reference(x):
    return {"y": np.broadcast_to(x[ROOT], x.shape)}

@@ -1,0 +1,70 @@
+from concourse.bass import DstId, RemoteDMATransfer
+
+K = [48, 48, 32]
+R = len(K)
+ROOT = 16
+HELPERS = [18, 19, 22, 23]
+CHIP3 = [24, 25, 26, 27, 28, 29, 30, 31]
+FAR0, FAR1 = 0, 8
+
+SCRATCH = dict(("d%d" % r, ("dram", [8, 128, K[r]], "float32")) for r in range(R))
+SEMAPHORES = ["%s%d" % (n, r) for n in ("ld", "h", "m", "a") for r in range(R)] + ["sent", "st"]
+
+
+def rank_program(g, core, T, topo):
+    def dst(c):
+        rid, pid, _se = topo.addr(c)
+        return DstId(rid=rid, pnc=pid)
+
+    def sem(n, r):
+        return T.sem["%s%d" % (n, r)]
+
+    def buf(r):
+        return T["d%d" % r]
+
+    def xfer(r, j, to, mask, s):
+        return RemoteDMATransfer(dst_ids=[dst(c) for c in to], dma_engine_mask=mask, remote_sem=s,
+                                 srcs=[buf(r)[j]], dsts=[buf(r)[j] for _c in to])
+
+    row0 = [sum(K[:r]) for r in range(R)]
+
+    def store(waits):
+        for r in range(R):
+            for n, v in waits:
+                g.sync.wait_ge(sem(n, r), v)
+            g.sync.dma_start(T.y[row0[r]:row0[r] + K[r], :], buf(r)[:]).then_inc(T.sem.st, 16)
+        g.sync.wait_ge(T.sem.st, 16 * R)
+
+    if core == ROOT:
+        for r in range(R):
+            q = g.sync if r % 2 == 0 else g.scalar
+            q.dma_start(buf(r)[:], T.x[row0[r]:row0[r] + K[r], :]).then_inc(sem("ld", r), 16)
+        for r in range(R):
+            g.wait_ge(sem("ld", r), 16)
+            g.remote_dma_fused([xfer(r, j, [HELPERS[j // 2]], 3 << (2 * j), sem("h", r)) for j in range(8)],
+                               local_sem=T.sem.sent)
+        g.scalar.wait_ge(T.sem.sent, 16 * R)
+        g.scalar.dma_start(T.y[:, :], T.x[:, :]).then_inc(T.sem.st, 16)
+        g.scalar.wait_ge(T.sem.st, 16)
+        g.wait_ge(T.sem.sent, 16 * R)
+    elif core in HELPERS:
+        j0 = 2 * HELPERS.index(core)
+        for r in range(R):
+            g.wait_ge(sem("h", r), 4)
+            g.remote_dma_fused([xfer(r, j0 + i, [CHIP3[j0 + i], FAR0], 0x0F << (4 * i), sem("m", r))
+                                for i in range(2)], local_sem=T.sem.sent)
+        g.wait_ge(T.sem.sent, 8 * R)
+    elif core in CHIP3:
+        j = CHIP3.index(core)
+        near = [c for c in CHIP3 if c != core and topo.die(c) == topo.die(core)]
+        over = [c for c in CHIP3 if topo.die(c) != topo.die(core)]
+        for r in range(R):
+            g.wait_ge(sem("m", r), 4)
+            g.remote_dma_fused([xfer(r, j, [FAR1] + near, 0x00FF, sem("a", r)),
+                                xfer(r, j, over, 0xFF00, sem("a", r))], local_sem=T.sem.sent)
+        store([("m", 4), ("a", 56)])
+        g.wait_ge(T.sem.sent, 16 * R)
+    elif core == FAR0:
+        store([("m", 32)])
+    elif core == FAR1:
+        store([("a", 64)])

@@ -1,14 +1,15 @@
 from concourse.bass import DstId, RemoteDMATransfer
 
-K = [48, 48, 32]
+K = [32, 32, 24, 24, 16]
 R = len(K)
 ROOT = 16
 HELPERS = [18, 19, 22, 23]
+GROUPS = [[0, 1, 2, 3]]
 CHIP3 = [24, 25, 26, 27, 28, 29, 30, 31]
 FAR0, FAR1 = 0, 8
 
-SCRATCH = dict(("d%d" % r, ("dram", [8, 128, K[r]], "float32")) for r in range(R))
-SEMAPHORES = ["%s%d" % (n, r) for n in ("ld", "h", "m", "a") for r in range(R)] + ["sent", "st"]
+SCRATCH = dict(("d%d" % r, ("dram", [4, 128, 2 * K[r]], "float32")) for r in range(R))
+SEMAPHORES = ["%s%d" % (n, r) for n in ("ld", "h", "m", "a") for r in range(R)] + ["sent", "st0", "st1"]
 
 
 def rank_program(g, core, T, topo):
@@ -22,18 +23,21 @@ def rank_program(g, core, T, topo):
     def buf(r):
         return T["d%d" % r]
 
-    def xfer(r, j, to, mask, s):
+    def xfer(r, h, to, mask, s):
         return RemoteDMATransfer(dst_ids=[dst(c) for c in to], dma_engine_mask=mask, remote_sem=s,
-                                 srcs=[buf(r)[j]], dsts=[buf(r)[j] for _c in to])
+                                 srcs=[buf(r)[h]], dsts=[buf(r)[h] for _c in to])
 
     row0 = [sum(K[:r]) for r in range(R)]
+    wide = 16 // len(GROUPS[0])
 
     def store(waits):
+        qs = (g.sync, g.scalar)
         for r in range(R):
-            for n, v in waits:
-                g.sync.wait_ge(sem(n, r), v)
-            g.sync.dma_start(T.y[row0[r]:row0[r] + K[r], :], buf(r)[:]).then_inc(T.sem.st, 16)
-        g.sync.wait_ge(T.sem.st, 16 * R)
+            for n, v in waits(r):
+                qs[r % 2].wait_ge(sem(n, r), v)
+            qs[r % 2].dma_start(T.y[row0[r]:row0[r] + K[r], :], buf(r)[:]).then_inc(T.sem["st%d" % (r % 2)], 16)
+        for i in range(min(2, R)):
+            qs[i].wait_ge(T.sem["st%d" % i], 16 * len(range(i, R, 2)))
 
     if core == ROOT:
         for r in range(R):
@@ -41,30 +45,33 @@ def rank_program(g, core, T, topo):
             q.dma_start(buf(r)[:], T.x[row0[r]:row0[r] + K[r], :]).then_inc(sem("ld", r), 16)
         for r in range(R):
             g.wait_ge(sem("ld", r), 16)
-            g.remote_dma_fused([xfer(r, j, [HELPERS[j // 2]], 3 << (2 * j), sem("h", r)) for j in range(8)],
-                               local_sem=T.sem.sent)
-        g.scalar.wait_ge(T.sem.sent, 16 * R)
-        g.scalar.dma_start(T.y[:, :], T.x[:, :]).then_inc(T.sem.st, 16)
-        g.scalar.wait_ge(T.sem.st, 16)
-        g.wait_ge(T.sem.sent, 16 * R)
+            for grp in GROUPS:
+                g.remote_dma_fused([xfer(r, h, [HELPERS[h]], ((1 << wide) - 1) << (wide * i), sem("h", r))
+                                    for i, h in enumerate(grp)], local_sem=T.sem.sent)
+        left = 16 * R * len(GROUPS)
+        g.scalar.wait_ge(T.sem.sent, left)
+        g.scalar.dma_start(T.y[:, :], T.x[:, :]).then_inc(T.sem.st0, 16)
+        g.scalar.wait_ge(T.sem.st0, 16)
+        g.wait_ge(T.sem.sent, left)
     elif core in HELPERS:
-        j0 = 2 * HELPERS.index(core)
+        h = HELPERS.index(core)
         for r in range(R):
-            g.wait_ge(sem("h", r), 4)
-            g.remote_dma_fused([xfer(r, j0 + i, [CHIP3[j0 + i], FAR0], 0x0F << (4 * i), sem("m", r))
-                                for i in range(2)], local_sem=T.sem.sent)
+            g.wait_ge(sem("h", r), wide)
+            g.remote_dma_fused([xfer(r, h, [CHIP3[2 * h + r % 2], FAR0], 0x00FF, sem("m", r))], local_sem=T.sem.sent)
         g.wait_ge(T.sem.sent, 8 * R)
     elif core in CHIP3:
         j = CHIP3.index(core)
         near = [c for c in CHIP3 if c != core and topo.die(c) == topo.die(core)]
         over = [c for c in CHIP3 if topo.die(c) != topo.die(core)]
-        for r in range(R):
-            g.wait_ge(sem("m", r), 4)
-            g.remote_dma_fused([xfer(r, j, [FAR1] + near, 0x00FF, sem("a", r)),
-                                xfer(r, j, over, 0xFF00, sem("a", r))], local_sem=T.sem.sent)
-        store([("m", 4), ("a", 56)])
-        g.wait_ge(T.sem.sent, 16 * R)
+        mine = [r for r in range(R) if r % 2 == j % 2]
+        for r in mine:
+            g.wait_ge(sem("m", r), 8)
+            g.remote_dma_fused([xfer(r, j // 2, [FAR1] + near, 0x00FF, sem("a", r)),
+                                xfer(r, j // 2, over, 0xFF00, sem("a", r))], local_sem=T.sem.sent)
+        store(lambda r: [("m", 8), ("a", 24)] if r in mine else [("a", 32)])
+        if mine:
+            g.wait_ge(T.sem.sent, 16 * len(mine))
     elif core == FAR0:
-        store([("m", 32)])
+        store(lambda r: [("m", 32)])
     elif core == FAR1:
-        store([("a", 64)])
+        store(lambda r: [("a", 32)])

from concourse.bass import DstId, RemoteDMATransfer

K = [32, 32, 24, 24, 16]
R = len(K)
ROOT = 16
HELPERS = [18, 19, 22, 23]
GROUPS = [[0, 1, 2, 3]]
CHIP3 = [24, 25, 26, 27, 28, 29, 30, 31]
FAR0, FAR1 = 0, 8

SCRATCH = dict(("d%d" % r, ("dram", [4, 128, 2 * K[r]], "float32")) for r in range(R))
SEMAPHORES = ["%s%d" % (n, r) for n in ("ld", "h", "m", "a") for r in range(R)] + ["sent", "st0", "st1"]


def rank_program(g, core, T, topo):
    def dst(c):
        rid, pid, _se = topo.addr(c)
        return DstId(rid=rid, pnc=pid)

    def sem(n, r):
        return T.sem["%s%d" % (n, r)]

    def buf(r):
        return T["d%d" % r]

    def xfer(r, h, to, mask, s):
        return RemoteDMATransfer(dst_ids=[dst(c) for c in to], dma_engine_mask=mask, remote_sem=s,
                                 srcs=[buf(r)[h]], dsts=[buf(r)[h] for _c in to])

    row0 = [sum(K[:r]) for r in range(R)]
    wide = 16 // len(GROUPS[0])

    def store(waits):
        qs = (g.sync, g.scalar)
        for r in range(R):
            for n, v in waits(r):
                qs[r % 2].wait_ge(sem(n, r), v)
            qs[r % 2].dma_start(T.y[row0[r]:row0[r] + K[r], :], buf(r)[:]).then_inc(T.sem["st%d" % (r % 2)], 16)
        for i in range(min(2, R)):
            qs[i].wait_ge(T.sem["st%d" % i], 16 * len(range(i, R, 2)))

    if core == ROOT:
        for r in range(R):
            q = g.sync if r % 2 == 0 else g.scalar
            q.dma_start(buf(r)[:], T.x[row0[r]:row0[r] + K[r], :]).then_inc(sem("ld", r), 16)
        for r in range(R):
            g.wait_ge(sem("ld", r), 16)
            for grp in GROUPS:
                g.remote_dma_fused([xfer(r, h, [HELPERS[h]], ((1 << wide) - 1) << (wide * i), sem("h", r))
                                    for i, h in enumerate(grp)], local_sem=T.sem.sent)
        left = 16 * R * len(GROUPS)
        g.scalar.wait_ge(T.sem.sent, left)
        g.scalar.dma_start(T.y[:, :], T.x[:, :]).then_inc(T.sem.st0, 16)
        g.scalar.wait_ge(T.sem.st0, 16)
        g.wait_ge(T.sem.sent, left)
    elif core in HELPERS:
        h = HELPERS.index(core)
        for r in range(R):
            g.wait_ge(sem("h", r), wide)
            g.remote_dma_fused([xfer(r, h, [CHIP3[2 * h + r % 2], FAR0], 0x00FF, sem("m", r))], local_sem=T.sem.sent)
        g.wait_ge(T.sem.sent, 8 * R)
    elif core in CHIP3:
        j = CHIP3.index(core)
        near = [c for c in CHIP3 if c != core and topo.die(c) == topo.die(core)]
        over = [c for c in CHIP3 if topo.die(c) != topo.die(core)]
        mine = [r for r in range(R) if r % 2 == j % 2]
        for r in mine:
            g.wait_ge(sem("m", r), 8)
            g.remote_dma_fused([xfer(r, j // 2, [FAR1] + near, 0x00FF, sem("a", r)),
                                xfer(r, j // 2, over, 0xFF00, sem("a", r))], local_sem=T.sem.sent)
        store(lambda r: [("m", 8), ("a", 24)] if r in mine else [("a", 32)])
        if mine:
            g.wait_ge(T.sem.sent, 16 * len(mine))
    elif core == FAR0:
        store(lambda r: [("m", 32)])
    elif core == FAR1:
        store(lambda r: [("a", 32)])
